import numpy as np
import ml_dtypes


def mxq(x, axis, fmt="e4m3"):
    dtype, down = {"e4m3": (ml_dtypes.float8_e4m3fn, 7), "e5m2": (ml_dtypes.float8_e5m2, 14)}[fmt]
    v = np.moveaxis(np.asarray(x, np.float32).astype(ml_dtypes.bfloat16).astype(np.float64), axis, -1)
    blocks = v.reshape(v.shape[:-1] + (-1, 32))
    amax = np.abs(blocks).max(-1, keepdims=True)
    byte = np.maximum(np.where(amax > 0, np.frexp(amax)[1] - 1 + 127, 0) - down, 1)
    scale = np.exp2(byte - 127.0)
    codes = (blocks / scale).astype(np.float32).astype(dtype).astype(np.float64)
    return np.moveaxis((codes * scale).reshape(v.shape), -1, axis)


WIDE = False


def mx_kscale(k):
    if not WIDE:
        return np.ones(k)
    levels = np.array([10, -10, 5, -5, 0])
    if k % 512:
        return np.exp2(np.random.permutation(np.resize(levels, k // 32))).repeat(32)
    a = np.empty((k // 512, 16))
    for p in range(k // 512):
        a[p, :8] = np.random.permutation(np.resize(levels, 8))
        for g in range(8):
            far = levels[np.abs(levels - a[p, g]) >= 10]
            a[p, g + 8] = far[np.random.randint(len(far))]
    return np.exp2(a.ravel()).repeat(32)


def f64(x):
    return np.asarray(x).astype(np.float64)


def striped(idx):
    return np.tile(idx.reshape(-1, 16).T, (8, 1)).astype(np.uint16)


def unstriped(offs):
    return offs[:16].T.reshape(-1).astype(np.int64)


K, T, E, C, N = 1024, 512, 6, 256, 384
TOP = 3


def by_expert(wq, xq):
    return np.concatenate([wq[e].T @ xq[:, e * C:(e + 1) * C] for e in range(E)], axis=1)


def setup_inputs():
    n = np.random.standard_normal
    s = mx_kscale(K)[:, None]
    deal = np.repeat(np.arange(E), C).reshape(TOP, T)[:, np.random.permutation(T)]
    deal = np.take_along_axis(deal, np.argsort(np.random.rand(TOP, T), axis=0), axis=0)
    for _ in range(8):
        s_, t_ = np.random.permutation(T).reshape(2, -1); r = np.random.randint(TOP, size=T // 2); x, y = deal[r, s_].copy(), deal[r, t_].copy()
        ok = ~((deal[:, s_] == y).any(0) | (deal[:, t_] == x).any(0)); deal[r[ok], s_[ok]] = y[ok]; deal[r[ok], t_[ok]] = x[ok]
    order = np.lexsort((np.random.rand(TOP * T), deal.reshape(-1)))
    slot_token = order % T; pos = np.empty(TOP * T, np.int64); pos[order] = np.arange(TOP * T); pos = pos.reshape(TOP, T)
    g = np.random.uniform(0.5, 1.5, (TOP, T)); g = g / g.sum(0)
    w_slot = np.empty(E * C)
    for r in range(TOP): w_slot[pos[r]] = g[r]
    return {
        "xT": (n((K, T)) * s).astype(np.float32),
        "w": (n((E, K, N)) / np.sqrt(K) / s[None]).astype(np.float32),
        "b": (0.3 * n((N, E))).astype(np.float32),
        "gate": np.tile(w_slot, (K, 1)).astype(np.float32),
        "offs": striped(slot_token),
        "pos1": striped(pos[0]),
        "pos2": striped(pos[1]),
        "pos3": striped(pos[2]),
    }


def reference(xT, w, b, gate, offs, pos1, pos2, pos3):
    idx = unstriped(offs)
    xq = mxq(f64(gate) * f64(xT)[:, idx], 0, "e4m3")
    y = by_expert(mxq(f64(w), 1, "e4m3"), xq)
    y = y + np.repeat(f64(b), C, axis=1)
    return y[:, unstriped(pos1)] + y[:, unstriped(pos2)] + y[:, unstriped(pos3)]

@@ -1,0 +1,242 @@
+from contextlib import ExitStack
+
+import concourse.mybir as mybir
+
+K, T, E, C, N = 1024, 512, 6, 256, 384
+S = E * C
+P = 128
+PACK = 4
+PASSES = K // (P * PACK)
+NT = N // P
+PAD = 16
+PAIR = 2 * C
+
+F32 = mybir.dt.float32
+BF16 = mybir.dt.bfloat16
+U32 = mybir.dt.uint32
+U16 = mybir.dt.uint16
+U8 = mybir.dt.uint8
+FP8X4 = mybir.dt.float8_e4m3fn_x4
+MULT = mybir.AluOpType.mult
+ADD = mybir.AluOpType.add
+IDENT = mybir.ActivationFunctionType.Identity
+
+FLOPS = 2 * S * K * N
+BYTES = 4 * (K * T + E * K * N + N * E + S + N * T) + 2 * P * (S + 3 * T) // 16
+
+
+def tile_moe_pre_lin_bias_kernel(tc, xT, w, b, gate, offs, pos1, pos2, pos3, out):
+    nc = tc.nc
+    with ExitStack() as ctx:
+        lists = ctx.enter_context(tc.tile_pool(name="lists", bufs=1))
+        keep = ctx.enter_context(tc.tile_pool(name="keep", bufs=1))
+        stage = ctx.enter_context(tc.tile_pool(name="stage", bufs=3))
+        rounded = ctx.enter_context(tc.tile_pool(name="rounded", bufs=2))
+        psum = ctx.enter_context(tc.psum_pool(name="psum", bufs=8))
+
+        offs_sb = lists.tile([P, S // 16], U16, name="offs_sb")
+        pos_sb = [lists.tile([P, T // 16], U16, name="pos%d_sb" % r) for r in range(3)]
+        gate_sb = keep.tile([P, S], F32, name="gate_sb")
+        bias_sb = keep.tile([P, NT, 8], F32, name="bias_sb")
+        planes = [[keep.tile([P, T + PAD], F32, name="x%d_%d" % (g, t)) for t in range(PACK)] for g in range(PASSES)]
+        w_raw = [keep.tile([P, PACK, N], F32, name="w%d" % i) for i in range(PASSES * E)]
+        w_bf = keep.tile([P, NT, PASSES * E, P, PACK], BF16, name="w_bf", align_bytes=64)
+        w_codes = keep.tile([P, NT, PASSES * E * P], U32, name="w_codes", align_bytes=64)
+        w_scales = keep.tile([P, NT, PASSES * E * P], U8, name="w_scales", align_bytes=64)
+        x_codes = keep.tile([P, PASSES, S], U32, name="x_codes", align_bytes=64)
+        x_scales = keep.tile([P, PASSES, S], U8, name="x_scales", align_bytes=64)
+        y = [keep.tile([P, S], F32, name="y%d" % nt) for nt in range(NT)]
+
+        x_rows = xT.rearrange("(g p t) c -> g t p c", p=P, t=PACK)
+        w_rows = w.rearrange("e (g p j) n -> g e p j n", p=P, j=PACK)
+
+        def load_plane(g, t):
+            nc.vector.memset(planes[g][t][:, T:], 0.0)
+            nc.sync.dma_start(out=planes[g][t][:, :T], in_=x_rows[g, t])
+
+        def load_gate(lo, hi):
+            nc.sync.dma_start(out=gate_sb[:, lo:hi], in_=gate[:P, lo:hi])
+
+        def load_w(i):
+            nc.sync.dma_start(out=w_raw[i][:], in_=w_rows[i // E, i % E])
+
+        nc.sync.dma_start(offs_sb[:], offs)
+        load_plane(0, 0)
+        load_gate(0, C)
+        for t in range(1, PACK):
+            load_plane(0, t)
+        load_gate(C, PAIR)
+        load_w(0)
+        load_gate(PAIR, 2 * PAIR)
+        load_w(1)
+        load_gate(2 * PAIR, S)
+        load_w(2)
+        load_w(3)
+        for t in range(PACK):
+            load_plane(1, t)
+        load_w(4)
+        load_w(5)
+        nc.sync.dma_start(out=bias_sb[:, :, :E], in_=b.rearrange("(c p) e -> p c e", p=P))
+        for tile, src in zip(pos_sb, (pos1, pos2, pos3)):
+            nc.sync.dma_start(tile[:], src)
+        for i in range(E, PASSES * E):
+            load_w(i)
+
+        def new_unit():
+            prod = stage.tile([P, PACK, PAIR], F32, name="stage")
+            x_bf = rounded.tile([P, PAIR, PACK], BF16, name="x_bf", align_bytes=64)
+            return prod, x_bf
+
+        def gather_x(unit, g, lo, hi):
+            prod, x_bf = unit
+            here = slice(lo % PAIR, lo % PAIR + hi - lo)
+            for t in range(PACK):
+                nc.vector.tensor_tensor(
+                    prod[:, t, here],
+                    planes[g][t][:].indirect(offs_sb[:, lo // 16 : hi // 16]),
+                    gate_sb[:, lo:hi],
+                    MULT,
+                )
+            nc.scalar.copy(
+                out=x_bf[:, here, :].rearrange("p (c i) t -> p c t i", i=4),
+                in_=prod[:, :, here].rearrange("p t (c i) -> p c t i", i=4),
+            )
+
+        def quantize_x(unit, g, lo, hi):
+            here = slice(lo % PAIR, lo % PAIR + hi - lo)
+            nc.vector.quantize_mx(
+                out=x_codes[:, g, lo:hi].bitcast(FP8X4),
+                scales=x_scales[:, g, lo:hi],
+                in_=unit[1][:, here, :].rearrange("p c t -> p (c t)"),
+            )
+
+        def round_w(i, tiles):
+            for nt in tiles:
+                nc.scalar.copy(
+                    out=w_bf[:, nt, i].rearrange("p (c i) j -> p c j i", i=4),
+                    in_=w_raw[i][:, :, nt * P : (nt + 1) * P].rearrange("p j (c i) -> p c j i", i=4),
+                )
+
+        def quantize_w(nt, grp):
+            cols = slice(grp * 4 * P, (grp + 1) * 4 * P)
+            nc.vector.quantize_mx(
+                out=w_codes[:, nt, cols].bitcast(FP8X4),
+                scales=w_scales[:, nt, cols],
+                in_=w_bf[:, nt, 4 * grp : 4 * grp + 4].rearrange("p i c j -> p (i c j)"),
+            )
+
+        def expert(nt, e, lo=0, hi=C):
+            acc = psum.tile([P, C], F32, name="acc")
+            slots = slice(e * C + lo, e * C + hi)
+            for g in range(PASSES):
+                cols = slice((g * E + e) * P, (g * E + e + 1) * P)
+                nc.tensor.matmul_mx(
+                    out=acc[:, lo:hi],
+                    lhsT=w_codes[:, nt, cols].bitcast(FP8X4),
+                    lhsT_scale=w_scales[:, nt, cols],
+                    rhs=x_codes[:, g, slots].bitcast(FP8X4),
+                    rhs_scale=x_scales[:, g, slots],
+                    start=(g == 0),
+                    stop=(g == PASSES - 1),
+                )
+            nc.scalar.activation(out=y[nt][:, slots], in_=acc[:, lo:hi], func=IDENT, bias=bias_sb[:, nt, e : e + 1])
+
+        def fetch(got, nt, r, a, z):
+            nc.vector.tensor_copy(got[:, r, a:z], y[nt][:].indirect(pos_sb[r][:, a // 16 : z // 16]))
+
+        def add_two(adder, got, a, z):
+            adder.tensor_tensor(got[:, 3, a:z], got[:, 0, a:z], got[:, 1, a:z], ADD)
+
+        def add_third(adder, got, nt, a, z):
+            adder.tensor_tensor(got[:, 0, a:z], got[:, 3, a:z], got[:, 2, a:z], ADD)
+            nc.sync.dma_start(out=out[nt * P : (nt + 1) * P, a:z], in_=got[:, 0, a:z])
+
+        every = range(NT)
+        u0 = new_unit()
+        gather_x(u0, 0, 0, C)
+        round_w(0, every)
+        gather_x(u0, 0, C, PAIR)
+        round_w(1, every)
+        round_w(2, every)
+        u1 = new_unit()
+        gather_x(u1, 0, PAIR, 2 * PAIR)
+        quantize_x(u0, 0, 0, PAIR)
+        round_w(3, every)
+        round_w(4, every)
+        u2 = new_unit()
+        gather_x(u2, 0, 2 * PAIR, S)
+        quantize_x(u1, 0, PAIR, 2 * PAIR)
+        round_w(5, every)
+        round_w(6, every)
+        u3 = new_unit()
+        gather_x(u3, 1, 0, PAIR)
+        quantize_x(u2, 0, 2 * PAIR, S)
+        quantize_w(0, 0)
+        for i in (7, 8, 9):
+            round_w(i, [0])
+        u4 = new_unit()
+        gather_x(u4, 1, PAIR, 2 * PAIR)
+        quantize_x(u3, 1, 0, PAIR)
+        quantize_w(0, 1)
+        round_w(10, [0])
+        round_w(11, [0])
+        expert(0, 0)
+        expert(0, 1)
+        round_w(7, [1])
+        u5 = new_unit()
+        gather_x(u5, 1, 2 * PAIR, S - C)
+        quantize_x(u4, 1, PAIR, 2 * PAIR)
+        quantize_w(0, 2)
+        expert(0, 2)
+        expert(0, 3)
+        round_w(8, [1])
+        gather_x(u5, 1, S - C, S)
+        quantize_x(u5, 1, 2 * PAIR, S - C)
+        expert(0, 4)
+        quantize_x(u5, 1, S - C, S)
+        expert(0, 5)
+        quantize_w(1, 0)
+        quantize_w(1, 1)
+        quantize_w(2, 0)
+        for i in (9, 10, 11):
+            round_w(i, [1])
+
+        def rest_of_tile_1():
+            quantize_w(1, 2)
+            for e in range(E):
+                expert(1, e)
+
+        def rest_of_tile_2():
+            for i in range(7, 12):
+                round_w(i, [2])
+            quantize_w(2, 1)
+            quantize_w(2, 2)
+            for e in range(E):
+                expert(2, e)
+
+        got0 = stage.tile([P, PACK, PAIR], F32, name="stage")
+        fetch(got0, 0, 0, 0, T)
+        fetch(got0, 0, 1, 0, T)
+        rest_of_tile_1()
+        fetch(got0, 0, 2, 0, T)
+        add_two(nc.vector, got0, 0, T)
+        got1 = stage.tile([P, PACK, PAIR], F32, name="stage")
+        fetch(got1, 1, 0, 0, T)
+        add_third(nc.vector, got0, 0, 0, T)
+        rest_of_tile_2()
+        fetch(got1, 1, 1, 0, T)
+        fetch(got1, 1, 2, 0, T)
+        add_two(nc.vector, got1, 0, T)
+        got2 = stage.tile([P, PACK, PAIR], F32, name="stage")
+        cut = 320
+        fetch(got2, 2, 0, 0, cut)
+        add_third(nc.vector, got1, 1, 0, T)
+        fetch(got2, 2, 1, 0, cut)
+        fetch(got2, 2, 0, cut, T)
+        add_two(nc.vector, got2, 0, cut)
+        fetch(got2, 2, 1, cut, T)
+        fetch(got2, 2, 2, 0, cut)
+        add_two(nc.vector, got2, cut, T)
+        add_third(nc.vector, got2, 2, 0, cut)
+        fetch(got2, 2, 2, cut, T)
+        add_third(nc.vector, got2, 2, cut, T)

@@ -30,213 +30,242 @@ def tile_moe_pre_lin_bias_kernel(tc, xT, w, b, gate, offs, pos1, pos2, pos3, out
     with ExitStack() as ctx:
         lists = ctx.enter_context(tc.tile_pool(name="lists", bufs=1))
         keep = ctx.enter_context(tc.tile_pool(name="keep", bufs=1))
-        stage = ctx.enter_context(tc.tile_pool(name="stage", bufs=3))
-        rounded = ctx.enter_context(tc.tile_pool(name="rounded", bufs=2))
         psum = ctx.enter_context(tc.psum_pool(name="psum", bufs=8))
+
+        def tile(shape, dtype, tag):
+            return keep.tile(shape, dtype, name=tag, tag=tag, align_bytes=64)
 
         offs_sb = lists.tile([P, S // 16], U16, name="offs_sb")
         pos_sb = [lists.tile([P, T // 16], U16, name="pos%d_sb" % r) for r in range(3)]
-        gate_sb = keep.tile([P, S], F32, name="gate_sb")
-        bias_sb = keep.tile([P, NT, 8], F32, name="bias_sb")
-        planes = [[keep.tile([P, T + PAD], F32, name="x%d_%d" % (g, t)) for t in range(PACK)] for g in range(PASSES)]
-        w_raw = [keep.tile([P, PACK, N], F32, name="w%d" % i) for i in range(PASSES * E)]
-        w_bf = keep.tile([P, NT, PASSES * E, P, PACK], BF16, name="w_bf", align_bytes=64)
-        w_codes = keep.tile([P, NT, PASSES * E * P], U32, name="w_codes", align_bytes=64)
-        w_scales = keep.tile([P, NT, PASSES * E * P], U8, name="w_scales", align_bytes=64)
-        x_codes = keep.tile([P, PASSES, S], U32, name="x_codes", align_bytes=64)
-        x_scales = keep.tile([P, PASSES, S], U8, name="x_scales", align_bytes=64)
-        y = [keep.tile([P, S], F32, name="y%d" % nt) for nt in range(NT)]
+        gate_a = tile([P, PAIR], F32, "gate_a")
+        gate_b = tile([P, 2 * PAIR], F32, "gate_b")
+        bias_sb = tile([P, NT, 8], F32, "bias")
+        planes = [[tile([P, 2 * PAIR + PAD], F32, "x%d_%d" % (g, t)) for t in range(PACK)] for g in range(PASSES)]
+        RING = 12
+        w_raw = [tile([P, PACK, N], F32, "w%d" % i) for i in range(RING)]
+        w_scales = tile([P, NT, PASSES * E * P], U8, "w_scales")
+        x_codes = tile([P, PASSES, S], U32, "x_codes")
+        x_scales = tile([P, PASSES, S], U8, "x_scales")
+        y = [tile([P, S], F32, "y%d" % nt) for nt in range(NT)]
+        narrow = {0: tile([P, PACK, PAIR], F32, "narrow")}
+        wide = [tile([P, PACK, 2 * PAIR], F32, "wide%d" % g) for g in range(PASSES)]
+        x_bf, w_bf, w_codes, got = {}, {}, {}, {}
 
         x_rows = xT.rearrange("(g p t) c -> g t p c", p=P, t=PACK)
         w_rows = w.rearrange("e (g p j) n -> g e p j n", p=P, j=PACK)
 
         def load_plane(g, t):
-            nc.vector.memset(planes[g][t][:, T:], 0.0)
             nc.sync.dma_start(out=planes[g][t][:, :T], in_=x_rows[g, t])
 
+        def gate_of(lo, hi):
+            return gate_a[:, lo:hi] if lo < PAIR else gate_b[:, lo - PAIR : hi - PAIR]
+
         def load_gate(lo, hi):
-            nc.sync.dma_start(out=gate_sb[:, lo:hi], in_=gate[:P, lo:hi])
+            nc.sync.dma_start(out=gate_of(lo, hi), in_=gate[:P, lo:hi])
 
         def load_w(i):
-            nc.sync.dma_start(out=w_raw[i][:], in_=w_rows[i // E, i % E])
+            nc.sync.dma_start(out=w_raw[i % RING][:], in_=w_rows[i // E, i % E])
 
-        nc.sync.dma_start(offs_sb[:], offs)
-        load_plane(0, 0)
-        load_gate(0, C)
-        for t in range(1, PACK):
-            load_plane(0, t)
-        load_gate(C, PAIR)
-        load_w(0)
-        load_gate(PAIR, 2 * PAIR)
-        load_w(1)
-        load_gate(2 * PAIR, S)
-        load_w(2)
-        load_w(3)
-        for t in range(PACK):
-            load_plane(1, t)
-        load_w(4)
-        load_w(5)
-        nc.sync.dma_start(out=bias_sb[:, :, :E], in_=b.rearrange("(c p) e -> p c e", p=P))
-        for tile, src in zip(pos_sb, (pos1, pos2, pos3)):
-            nc.sync.dma_start(tile[:], src)
-        for i in range(E, PASSES * E):
-            load_w(i)
+        def prod(g, lo, hi):
+            if lo >= PAIR:
+                return wide[g][:, :, lo - PAIR : hi - PAIR]
+            if g not in narrow:
+                narrow[g] = tile([P, PACK, PAIR], F32, "gate_b")
+            return narrow[g][:, :, lo:hi]
 
-        def new_unit():
-            prod = stage.tile([P, PACK, PAIR], F32, name="stage")
-            x_bf = rounded.tile([P, PAIR, PACK], BF16, name="x_bf", align_bytes=64)
-            return prod, x_bf
-
-        def gather_x(unit, g, lo, hi):
-            prod, x_bf = unit
-            here = slice(lo % PAIR, lo % PAIR + hi - lo)
-            for t in range(PACK):
-                nc.vector.tensor_tensor(
-                    prod[:, t, here],
-                    planes[g][t][:].indirect(offs_sb[:, lo // 16 : hi // 16]),
-                    gate_sb[:, lo:hi],
-                    MULT,
-                )
-            nc.scalar.copy(
-                out=x_bf[:, here, :].rearrange("p (c i) t -> p c t i", i=4),
-                in_=prod[:, :, here].rearrange("p t (c i) -> p c t i", i=4),
+        def gather(g, t, lo, hi):
+            nc.vector.tensor_tensor(
+                prod(g, lo, hi)[:, t, :],
+                planes[g][t][:].indirect(offs_sb[:, lo // 16 : hi // 16]),
+                gate_of(lo, hi),
+                MULT,
             )
 
-        def quantize_x(unit, g, lo, hi):
-            here = slice(lo % PAIR, lo % PAIR + hi - lo)
+        def gather_x(g, lo, hi):
+            for t in range(PACK):
+                gather(g, t, lo, hi)
+
+        x_tag = {(0, False): "xbf", (0, True): "w3", (1, True): "narrow", (1, False): "xbf"}
+
+        def rounded(g, lo, hi):
+            key = (g, lo >= PAIR)
+            if key not in x_bf:
+                x_bf[key] = tile([P, 2 * PAIR if key[1] else PAIR, PACK], BF16, x_tag[key])
+            base = PAIR if key[1] else 0
+            return x_bf[key][:, lo - base : hi - base, :]
+
+        def round_x(g, lo, hi):
+            nc.scalar.copy(
+                out=rounded(g, lo, hi).rearrange("p (c i) t -> p c t i", i=4),
+                in_=prod(g, lo, hi).rearrange("p t (c i) -> p c t i", i=4),
+            )
+
+        def q_x(g, lo, hi):
             nc.vector.quantize_mx(
                 out=x_codes[:, g, lo:hi].bitcast(FP8X4),
                 scales=x_scales[:, g, lo:hi],
-                in_=unit[1][:, here, :].rearrange("p c t -> p (c t)"),
+                in_=rounded(g, lo, hi).rearrange("p c t -> p (c t)"),
             )
 
-        def round_w(i, tiles):
+        bf_tag = {(nt, grp): "wbf%d_%d" % (nt, grp) for nt in range(NT) for grp in range(2)}
+        bf_tag[(2, 1)] = bf_tag[(0, 0)]
+        bf_tag[(2, 2)] = bf_tag[(0, 1)]
+
+        def cast_w(i, tiles, copy=nc.scalar.copy):
             for nt in tiles:
-                nc.scalar.copy(
-                    out=w_bf[:, nt, i].rearrange("p (c i) j -> p c j i", i=4),
+                if (nt, i // 4) not in w_bf:
+                    if (nt, i // 4) in bf_tag:
+                        w_bf[(nt, i // 4)] = tile([P, PAIR, PACK], BF16, bf_tag[(nt, i // 4)])[:]
+                    else:
+                        both = tile([P, 2, PAIR, PACK], BF16, "wide0")
+                        w_bf[(0, 2)] = both[:, 0]
+                        w_bf[(1, 2)] = both[:, 1]
+                copy(
+                    out=w_bf[(nt, i // 4)][:, (i % 4) * P : (i % 4 + 1) * P, :].rearrange("p (c i) j -> p c j i", i=4),
                     in_=w_raw[i][:, :, nt * P : (nt + 1) * P].rearrange("p j (c i) -> p c j i", i=4),
                 )
 
-        def quantize_w(nt, grp):
-            cols = slice(grp * 4 * P, (grp + 1) * 4 * P)
+        def quantize_w(nt, grp, tag):
+            w_codes[(nt, grp)] = tile([P, 4 * P], U32, tag)
             nc.vector.quantize_mx(
-                out=w_codes[:, nt, cols].bitcast(FP8X4),
-                scales=w_scales[:, nt, cols],
-                in_=w_bf[:, nt, 4 * grp : 4 * grp + 4].rearrange("p i c j -> p (i c j)"),
+                out=w_codes[(nt, grp)][:].bitcast(FP8X4),
+                scales=w_scales[:, nt, grp * 4 * P : (grp + 1) * 4 * P],
+                in_=w_bf[(nt, grp)].rearrange("p c j -> p (c j)"),
             )
 
-        def expert(nt, e, lo=0, hi=C):
+        def expert(nt, e):
             acc = psum.tile([P, C], F32, name="acc")
-            slots = slice(e * C + lo, e * C + hi)
+            slots = slice(e * C, (e + 1) * C)
             for g in range(PASSES):
-                cols = slice((g * E + e) * P, (g * E + e + 1) * P)
+                i = g * E + e
                 nc.tensor.matmul_mx(
-                    out=acc[:, lo:hi],
-                    lhsT=w_codes[:, nt, cols].bitcast(FP8X4),
-                    lhsT_scale=w_scales[:, nt, cols],
+                    out=acc[:],
+                    lhsT=w_codes[(nt, i // 4)][:, (i % 4) * P : (i % 4 + 1) * P].bitcast(FP8X4),
+                    lhsT_scale=w_scales[:, nt, i * P : (i + 1) * P],
                     rhs=x_codes[:, g, slots].bitcast(FP8X4),
                     rhs_scale=x_scales[:, g, slots],
                     start=(g == 0),
                     stop=(g == PASSES - 1),
                 )
-            nc.scalar.activation(out=y[nt][:, slots], in_=acc[:, lo:hi], func=IDENT, bias=bias_sb[:, nt, e : e + 1])
+            nc.scalar.activation(out=y[nt][:, slots], in_=acc[:], func=IDENT, bias=bias_sb[:, nt, e : e + 1])
 
-        def fetch(got, nt, r, a, z):
-            nc.vector.tensor_copy(got[:, r, a:z], y[nt][:].indirect(pos_sb[r][:, a // 16 : z // 16]))
+        def room(nt, tag_a, tag_b):
+            a = tile([P, 2, T], F32, tag_a)
+            z = tile([P, 2, T], F32, tag_b)
+            got[nt] = [a[:, 0, :], z[:, 0, :], z[:, 1, :], a[:, 1, :]]
 
-        def add_two(adder, got, a, z):
-            adder.tensor_tensor(got[:, 3, a:z], got[:, 0, a:z], got[:, 1, a:z], ADD)
+        def fetch(nt, r, a, z):
+            nc.vector.tensor_copy(got[nt][r][:, a:z], y[nt][:].indirect(pos_sb[r][:, a // 16 : z // 16]))
 
-        def add_third(adder, got, nt, a, z):
-            adder.tensor_tensor(got[:, 0, a:z], got[:, 3, a:z], got[:, 2, a:z], ADD)
-            nc.sync.dma_start(out=out[nt * P : (nt + 1) * P, a:z], in_=got[:, 0, a:z])
+        def add_two(adder, nt):
+            adder.tensor_tensor(got[nt][3], got[nt][0], got[nt][1], ADD)
 
-        every = range(NT)
-        u0 = new_unit()
-        gather_x(u0, 0, 0, C)
-        round_w(0, every)
-        gather_x(u0, 0, C, PAIR)
-        round_w(1, every)
-        round_w(2, every)
-        u1 = new_unit()
-        gather_x(u1, 0, PAIR, 2 * PAIR)
-        quantize_x(u0, 0, 0, PAIR)
-        round_w(3, every)
-        round_w(4, every)
-        u2 = new_unit()
-        gather_x(u2, 0, 2 * PAIR, S)
-        quantize_x(u1, 0, PAIR, 2 * PAIR)
-        round_w(5, every)
-        round_w(6, every)
-        u3 = new_unit()
-        gather_x(u3, 1, 0, PAIR)
-        quantize_x(u2, 0, 2 * PAIR, S)
-        quantize_w(0, 0)
-        for i in (7, 8, 9):
-            round_w(i, [0])
-        u4 = new_unit()
-        gather_x(u4, 1, PAIR, 2 * PAIR)
-        quantize_x(u3, 1, 0, PAIR)
-        quantize_w(0, 1)
-        round_w(10, [0])
-        round_w(11, [0])
+        def add_third(adder, nt, a, z):
+            adder.tensor_tensor(got[nt][0][:, a:z], got[nt][3][:, a:z], got[nt][2][:, a:z], ADD)
+            nc.sync.dma_start(out=out[nt * P : (nt + 1) * P, a:z], in_=got[nt][0][:, a:z])
+
+        nc.sync.dma_start(offs_sb[:], offs)
+        load_plane(0, 0)
+        load_gate(0, PAIR)
+        load_plane(0, 1)
+        nc.sync.dma_start(out=w_raw[0][:, :, :P], in_=w_rows[0, 0][:, :, :P])
+        load_plane(0, 2)
+        nc.sync.dma_start(out=w_raw[0][:, :, P:], in_=w_rows[0, 0][:, :, P:])
+        load_plane(0, 3)
+        load_gate(PAIR, S)
+        load_w(1)
+        load_w(2)
+        load_w(3)
+        load_plane(1, 0)
+        load_w(4)
+        load_plane(1, 1)
+        load_w(5)
+        load_w(6)
+        load_plane(1, 2)
+        load_w(7)
+        load_w(8)
+        load_plane(1, 3)
+        load_w(9)
+        load_w(10)
+        load_w(11)
+        nc.sync.dma_start(out=bias_sb[:, :, :E], in_=b.rearrange("(c p) e -> p c e", p=P))
+        nc.sync.dma_start(pos_sb[0][:], pos1)
+        nc.sync.dma_start(pos_sb[1][:], pos2)
+        nc.sync.dma_start(pos_sb[2][:], pos3)
+
+        gather_x(0, 0, PAIR)
+        cast_w(0, [0, 1, 2])
+        round_x(0, 0, 512)
+        gather_x(0, PAIR, S)
+        q_x(0, 0, 512)
+        for i in range(1, 4):
+            cast_w(i, [0, 1, 2])
+        cast_w(4, [0, 1])
+        round_x(0, 512, 1024)
+        round_x(0, 1024, S)
+        gather(1, 0, PAIR, S)
+        gather(1, 1, PAIR, S)
+        q_x(0, 512, 1024)
+        gather(1, 2, PAIR, S)
+        q_x(0, 1024, S)
+        gather(1, 3, PAIR, S)
+        for i in range(5, 11):
+            cast_w(i, [0, 1] if i < 12 else [0])
+        round_x(1, 512, 1024)
+        cast_w(11, [0, 1] if 11 < 12 else [0])
+        round_x(1, 1024, S)
+        gather_x(1, 0, PAIR)
+        quantize_w(0, 0, "x1_0")
+        quantize_w(0, 1, "x1_1")
+        quantize_w(0, 2, "wc0_2")
+        q_x(1, 512, 1024)
+        q_x(1, 1024, S)
+        round_x(1, 0, C)
+        round_x(1, C, PAIR)
+        for e in range(2, E):
+            expert(0, e)
+        q_x(1, 0, C)
         expert(0, 0)
+        q_x(1, C, PAIR)
         expert(0, 1)
-        round_w(7, [1])
-        u5 = new_unit()
-        gather_x(u5, 1, 2 * PAIR, S - C)
-        quantize_x(u4, 1, PAIR, 2 * PAIR)
-        quantize_w(0, 2)
-        expert(0, 2)
-        expert(0, 3)
-        round_w(8, [1])
-        gather_x(u5, 1, S - C, S)
-        quantize_x(u5, 1, 2 * PAIR, S - C)
-        expert(0, 4)
-        quantize_x(u5, 1, S - C, S)
-        expert(0, 5)
-        quantize_w(1, 0)
-        quantize_w(1, 1)
-        quantize_w(2, 0)
-        for i in (9, 10, 11):
-            round_w(i, [1])
-
-        def rest_of_tile_1():
-            quantize_w(1, 2)
-            for e in range(E):
-                expert(1, e)
-
-        def rest_of_tile_2():
-            for i in range(7, 12):
-                round_w(i, [2])
-            quantize_w(2, 1)
-            quantize_w(2, 2)
-            for e in range(E):
-                expert(2, e)
-
-        got0 = stage.tile([P, PACK, PAIR], F32, name="stage")
-        fetch(got0, 0, 0, 0, T)
-        fetch(got0, 0, 1, 0, T)
-        rest_of_tile_1()
-        fetch(got0, 0, 2, 0, T)
-        add_two(nc.vector, got0, 0, T)
-        got1 = stage.tile([P, PACK, PAIR], F32, name="stage")
-        fetch(got1, 1, 0, 0, T)
-        add_third(nc.vector, got0, 0, 0, T)
-        rest_of_tile_2()
-        fetch(got1, 1, 1, 0, T)
-        fetch(got1, 1, 2, 0, T)
-        add_two(nc.vector, got1, 0, T)
-        got2 = stage.tile([P, PACK, PAIR], F32, name="stage")
+        quantize_w(1, 0, "x1_2")
+        quantize_w(1, 1, "x1_3")
+        quantize_w(2, 0, "gate_a")
+        for i in range(12, 12):
+            cast_w(i, [1])
+        expert(1, 0)
+        expert(1, 1)
+        quantize_w(1, 2, "wc1_2")
+        for e in range(2, E):
+            expert(1, e)
+        room(0, "x0_0", "wide0")
+        fetch(0, 0, 0, T)
+        fetch(0, 1, 0, T)
+        add_two(nc.gpsimd, 0)
+        fetch(0, 2, 0, T)
+        add_third(nc.gpsimd, 0, 0, T)
+        for i in range(4, 12 - 4):
+            cast_w(i, [2])
+        for i in range(12 - 4, 12):
+            cast_w(i, [2], nc.vector.tensor_copy)
+        quantize_w(2, 1, "wc2_1")
+        expert(2, 0)
+        expert(2, 1)
+        quantize_w(2, 2, "wc2_2")
+        for e in range(2, E):
+            expert(2, e)
+        room(1, "x0_1", "wbf0_0")
+        fetch(1, 0, 0, T)
+        fetch(1, 1, 0, T)
+        add_two(nc.gpsimd, 1)
+        fetch(1, 2, 0, T)
+        add_third(nc.gpsimd, 1, 0, T)
         cut = 320
-        fetch(got2, 2, 0, 0, cut)
-        add_third(nc.vector, got1, 1, 0, T)
-        fetch(got2, 2, 1, 0, cut)
-        fetch(got2, 2, 0, cut, T)
-        add_two(nc.vector, got2, 0, cut)
-        fetch(got2, 2, 1, cut, T)
-        fetch(got2, 2, 2, 0, cut)
-        add_two(nc.vector, got2, cut, T)
-        add_third(nc.vector, got2, 2, 0, cut)
-        fetch(got2, 2, 2, cut, T)
-        add_third(nc.vector, got2, 2, cut, T)
+        room(2, "x0_2", "x0_3")
+        fetch(2, 0, 0, T)
+        fetch(2, 1, 0, T)
+        add_two(nc.gpsimd, 2)
+        fetch(2, 2, 0, cut)
+        fetch(2, 2, cut, T)
+        add_third(nc.vector, 2, 0, cut)
+        add_third(nc.vector, 2, cut, T)

@@ -41,15 +41,15 @@ def tile_moe_pre_lin_bias_kernel(tc, xT, w, b, gate, offs, pos1, pos2, pos3, out
         gate_b = tile([P, 2 * PAIR], F32, "gate_b")
         bias_sb = tile([P, NT, 8], F32, "bias")
         planes = [[tile([P, 2 * PAIR + PAD], F32, "x%d_%d" % (g, t)) for t in range(PACK)] for g in range(PASSES)]
-        RING = 12
-        w_raw = [tile([P, PACK, N], F32, "w%d" % i) for i in range(RING)]
-        w_scales = tile([P, NT, PASSES * E * P], U8, "w_scales")
+        SPLIT = 0
+        w_ab = [tile([P, PACK, N if i < SPLIT else 2 * P], F32, "w%d" % i) for i in range(PASSES * E)]
+        w_c = {i: tile([P, PACK, P], F32, "wc%d" % i) for i in range(SPLIT, PASSES * E)}
         x_codes = tile([P, PASSES, S], U32, "x_codes")
         x_scales = tile([P, PASSES, S], U8, "x_scales")
         y = [tile([P, S], F32, "y%d" % nt) for nt in range(NT)]
         narrow = {0: tile([P, PACK, PAIR], F32, "narrow")}
         wide = [tile([P, PACK, 2 * PAIR], F32, "wide%d" % g) for g in range(PASSES)]
-        x_bf, w_bf, w_codes, got = {}, {}, {}, {}
+        x_bf, w_bf, w_codes, w_scales, got = {}, {}, {}, {}, {}
 
         x_rows = xT.rearrange("(g p t) c -> g t p c", p=P, t=PACK)
         w_rows = w.rearrange("e (g p j) n -> g e p j n", p=P, j=PACK)
@@ -63,8 +63,11 @@ def tile_moe_pre_lin_bias_kernel(tc, xT, w, b, gate, offs, pos1, pos2, pos3, out
         def load_gate(lo, hi):
             nc.sync.dma_start(out=gate_of(lo, hi), in_=gate[:P, lo:hi])
 
-        def load_w(i):
-            nc.sync.dma_start(out=w_raw[i % RING][:], in_=w_rows[i // E, i % E])
+        def raw(i, lo, hi):
+            return w_c[i][:, :, lo - 2 * P : hi - 2 * P] if i >= SPLIT and lo >= 2 * P else w_ab[i][:, :, lo:hi]
+
+        def load_w(i, lo, hi):
+            nc.sync.dma_start(out=raw(i, lo, hi), in_=w_rows[i // E, i % E][:, :, lo:hi])
 
         def prod(g, lo, hi):
             if lo >= PAIR:
@@ -85,7 +88,7 @@ def tile_moe_pre_lin_bias_kernel(tc, xT, w, b, gate, offs, pos1, pos2, pos3, out
             for t in range(PACK):
                 gather(g, t, lo, hi)
 
-        x_tag = {(0, False): "xbf", (0, True): "w3", (1, True): "narrow", (1, False): "xbf"}
+        x_tag = {(0, False): "xbf", (0, True): "w6", (1, True): "narrow", (1, False): "xbf"}
 
         def rounded(g, lo, hi):
             key = (g, lo >= PAIR)
@@ -107,41 +110,55 @@ def tile_moe_pre_lin_bias_kernel(tc, xT, w, b, gate, offs, pos1, pos2, pos3, out
                 in_=rounded(g, lo, hi).rearrange("p c t -> p (c t)"),
             )
 
-        bf_tag = {(nt, grp): "wbf%d_%d" % (nt, grp) for nt in range(NT) for grp in range(2)}
-        bf_tag[(2, 1)] = bf_tag[(0, 0)]
-        bf_tag[(2, 2)] = bf_tag[(0, 1)]
+        batches = [
+            ([(0, i) for i in range(8)], "b0", "x1_0"),
+            ([(1, i) for i in range(8)], "b1", "xbf"),
+            ([(nt, i) for nt in (0, 1) for i in range(8, 12)], "wide0", "x1_1"),
+            ([(2, i) for i in (0, 6)], "b3", "b1"),
+            ([(2, i) for i in (1, 7, 2, 8)], "b3", "x1_2"),
+            ([(2, i) for i in (3, 9, 4, 10, 5, 11)], "narrow", "x1_3"),
+        ]
+        place = {block: (n, at * P) for n, batch in enumerate(batches) for at, block in enumerate(batch[0])}
+
+        def w_target(nt, i):
+            n, at = place[(nt, i)]
+            if n not in w_bf:
+                w_bf[n] = tile([P, len(batches[n][0]) * P, PACK], BF16, batches[n][1])
+            return w_bf[n][:, at : at + P, :]
 
         def cast_w(i, tiles, copy=nc.scalar.copy):
             for nt in tiles:
-                if (nt, i // 4) not in w_bf:
-                    if (nt, i // 4) in bf_tag:
-                        w_bf[(nt, i // 4)] = tile([P, PAIR, PACK], BF16, bf_tag[(nt, i // 4)])[:]
-                    else:
-                        both = tile([P, 2, PAIR, PACK], BF16, "wide0")
-                        w_bf[(0, 2)] = both[:, 0]
-                        w_bf[(1, 2)] = both[:, 1]
                 copy(
-                    out=w_bf[(nt, i // 4)][:, (i % 4) * P : (i % 4 + 1) * P, :].rearrange("p (c i) j -> p c j i", i=4),
-                    in_=w_raw[i][:, :, nt * P : (nt + 1) * P].rearrange("p j (c i) -> p c j i", i=4),
+                    out=w_target(nt, i).rearrange("p (c i) j -> p c j i", i=4),
+                    in_=raw(i, nt * P, (nt + 1) * P).rearrange("p j (c i) -> p c j i", i=4),
                 )
 
-        def quantize_w(nt, grp, tag):
-            w_codes[(nt, grp)] = tile([P, 4 * P], U32, tag)
+        def cast_w_gpsimd(i, nt):
+            nc.gpsimd.tensor_scalar(
+                w_target(nt, i), raw(i, nt * P, (nt + 1) * P).rearrange("p j c -> p c j"), 1.0, 0.0, MULT, ADD
+            )
+
+        def quantize_w(n, lo=0, hi=None):
+            width = len(batches[n][0]) * P
+            if n not in w_codes:
+                w_codes[n] = tile([P, width], U32, batches[n][2])
+                w_scales[n] = tile([P, width], U8, "ws%d" % n)
+            cols = slice(lo * P, hi * P if hi else width)
             nc.vector.quantize_mx(
-                out=w_codes[(nt, grp)][:].bitcast(FP8X4),
-                scales=w_scales[:, nt, grp * 4 * P : (grp + 1) * 4 * P],
-                in_=w_bf[(nt, grp)].rearrange("p c j -> p (c j)"),
+                out=w_codes[n][:, cols].bitcast(FP8X4),
+                scales=w_scales[n][:, cols],
+                in_=w_bf[n][:, cols, :].rearrange("p c j -> p (c j)"),
             )
 
         def expert(nt, e):
             acc = psum.tile([P, C], F32, name="acc")
             slots = slice(e * C, (e + 1) * C)
             for g in range(PASSES):
-                i = g * E + e
+                n, at = place[(nt, g * E + e)]
                 nc.tensor.matmul_mx(
                     out=acc[:],
-                    lhsT=w_codes[(nt, i // 4)][:, (i % 4) * P : (i % 4 + 1) * P].bitcast(FP8X4),
-                    lhsT_scale=w_scales[:, nt, i * P : (i + 1) * P],
+                    lhsT=w_codes[n][:, at : at + P].bitcast(FP8X4),
+                    lhsT_scale=w_scales[n][:, at : at + P],
                     rhs=x_codes[:, g, slots].bitcast(FP8X4),
                     rhs_scale=x_scales[:, g, slots],
                     start=(g == 0),
@@ -149,77 +166,82 @@ def tile_moe_pre_lin_bias_kernel(tc, xT, w, b, gate, offs, pos1, pos2, pos3, out
                 )
             nc.scalar.activation(out=y[nt][:, slots], in_=acc[:], func=IDENT, bias=bias_sb[:, nt, e : e + 1])
 
-        def room(nt, tag_a, tag_b):
-            a = tile([P, 2, T], F32, tag_a)
-            z = tile([P, 2, T], F32, tag_b)
-            got[nt] = [a[:, 0, :], z[:, 0, :], z[:, 1, :], a[:, 1, :]]
-
         def fetch(nt, r, a, z):
             nc.vector.tensor_copy(got[nt][r][:, a:z], y[nt][:].indirect(pos_sb[r][:, a // 16 : z // 16]))
 
-        def add_two(adder, nt):
-            adder.tensor_tensor(got[nt][3], got[nt][0], got[nt][1], ADD)
+        def add_two(adder, nt, a=0, z=T):
+            adder.tensor_tensor(got[nt][3][:, a:z], got[nt][0][:, a:z], got[nt][1][:, a:z], ADD)
 
         def add_third(adder, nt, a, z):
-            adder.tensor_tensor(got[nt][0][:, a:z], got[nt][3][:, a:z], got[nt][2][:, a:z], ADD)
-            nc.sync.dma_start(out=out[nt * P : (nt + 1) * P, a:z], in_=got[nt][0][:, a:z])
+            adder.tensor_tensor(got[nt][4][:, a:z], got[nt][3][:, a:z], got[nt][2][:, a:z], ADD)
+            nc.sync.dma_start(out=out[nt * P : (nt + 1) * P, a:z], in_=got[nt][4][:, a:z])
 
         nc.sync.dma_start(offs_sb[:], offs)
         load_plane(0, 0)
         load_gate(0, PAIR)
         load_plane(0, 1)
-        nc.sync.dma_start(out=w_raw[0][:, :, :P], in_=w_rows[0, 0][:, :, :P])
+        load_w(0, 0 * P, 1 * P)
         load_plane(0, 2)
-        nc.sync.dma_start(out=w_raw[0][:, :, P:], in_=w_rows[0, 0][:, :, P:])
+        load_w(0, 1 * P, 2 * P)
+        load_w(0, 2 * P, 3 * P)
         load_plane(0, 3)
         load_gate(PAIR, S)
-        load_w(1)
-        load_w(2)
-        load_w(3)
+        load_w(1, 0, 2 * P)
+        load_w(2, 0, 2 * P)
+        load_w(3, 0, 2 * P)
+        load_w(4, 0, 2 * P)
         load_plane(1, 0)
-        load_w(4)
+        load_w(5, 0, 2 * P)
+        load_w(6, 0, 2 * P)
         load_plane(1, 1)
-        load_w(5)
-        load_w(6)
+        load_w(6, 2 * P, 3 * P)
+        load_w(7, 0, 2 * P)
         load_plane(1, 2)
-        load_w(7)
-        load_w(8)
+        load_w(8, 0, 2 * P)
+        load_w(9, 0, 2 * P)
         load_plane(1, 3)
-        load_w(9)
-        load_w(10)
-        load_w(11)
+        load_w(10, 0, 2 * P)
+        load_w(11, 0, 2 * P)
         nc.sync.dma_start(out=bias_sb[:, :, :E], in_=b.rearrange("(c p) e -> p c e", p=P))
         nc.sync.dma_start(pos_sb[0][:], pos1)
         nc.sync.dma_start(pos_sb[1][:], pos2)
         nc.sync.dma_start(pos_sb[2][:], pos3)
+        load_w(1, 2 * P, 3 * P)
+        load_w(7, 2 * P, 3 * P)
+        load_w(2, 2 * P, 3 * P)
+        load_w(8, 2 * P, 3 * P)
+        load_w(3, 2 * P, 3 * P)
+        load_w(9, 2 * P, 3 * P)
+        load_w(4, 2 * P, 3 * P)
+        load_w(10, 2 * P, 3 * P)
+        load_w(5, 2 * P, 3 * P)
+        load_w(11, 2 * P, 3 * P)
 
         gather_x(0, 0, PAIR)
         cast_w(0, [0, 1, 2])
-        round_x(0, 0, 512)
+        round_x(0, 0, PAIR)
         gather_x(0, PAIR, S)
-        q_x(0, 0, 512)
-        for i in range(1, 4):
-            cast_w(i, [0, 1, 2])
-        cast_w(4, [0, 1])
-        round_x(0, 512, 1024)
-        round_x(0, 1024, S)
+        q_x(0, 0, PAIR)
+        for i in range(1, 7):
+            cast_w(i, [0, 1])
+        round_x(0, PAIR, 2 * PAIR)
+        round_x(0, 2 * PAIR, S)
+        cast_w(6, [2])
         gather(1, 0, PAIR, S)
         gather(1, 1, PAIR, S)
-        q_x(0, 512, 1024)
+        q_x(0, PAIR, 2 * PAIR)
         gather(1, 2, PAIR, S)
-        q_x(0, 1024, S)
+        q_x(0, 2 * PAIR, S)
         gather(1, 3, PAIR, S)
-        for i in range(5, 11):
-            cast_w(i, [0, 1] if i < 12 else [0])
-        round_x(1, 512, 1024)
-        cast_w(11, [0, 1] if 11 < 12 else [0])
-        round_x(1, 1024, S)
+        for i in range(7, 12):
+            cast_w(i, [0, 1, 2] if i == 6 else [0, 1])
+        round_x(1, PAIR, 2 * PAIR)
+        round_x(1, 2 * PAIR, S)
         gather_x(1, 0, PAIR)
-        quantize_w(0, 0, "x1_0")
-        quantize_w(0, 1, "x1_1")
-        quantize_w(0, 2, "wc0_2")
-        q_x(1, 512, 1024)
-        q_x(1, 1024, S)
+        quantize_w(0)
+        quantize_w(2)
+        q_x(1, PAIR, 2 * PAIR)
+        q_x(1, 2 * PAIR, S)
         round_x(1, 0, C)
         round_x(1, C, PAIR)
         for e in range(2, E):
@@ -228,43 +250,45 @@ def tile_moe_pre_lin_bias_kernel(tc, xT, w, b, gate, offs, pos1, pos2, pos3, out
         expert(0, 0)
         q_x(1, C, PAIR)
         expert(0, 1)
-        quantize_w(1, 0, "x1_2")
-        quantize_w(1, 1, "x1_3")
-        quantize_w(2, 0, "gate_a")
-        for i in range(12, 12):
-            cast_w(i, [1])
-        expert(1, 0)
-        expert(1, 1)
-        quantize_w(1, 2, "wc1_2")
-        for e in range(2, E):
+        quantize_w(1)
+        quantize_w(3)
+        for e in range(E):
             expert(1, e)
-        room(0, "x0_0", "wide0")
-        fetch(0, 0, 0, T)
-        fetch(0, 1, 0, T)
-        add_two(nc.gpsimd, 0)
-        fetch(0, 2, 0, T)
-        add_third(nc.gpsimd, 0, 0, T)
-        for i in range(4, 12 - 4):
+        for i in (1, 7, 2, 8):
+            cast_w_gpsimd(i, 2)
+        for i in (3, 9, 4, 10, 5, 11):
             cast_w(i, [2])
-        for i in range(12 - 4, 12):
-            cast_w(i, [2], nc.vector.tensor_copy)
-        quantize_w(2, 1, "wc2_1")
-        expert(2, 0)
-        expert(2, 1)
-        quantize_w(2, 2, "wc2_2")
-        for e in range(2, E):
-            expert(2, e)
-        room(1, "x0_1", "wbf0_0")
+        first = tile([P, 3, T], F32, "wide0")
+        got[0] = [first[:, r, :] for r in range(3)]
+        for r in range(3):
+            fetch(0, r, 0, T)
+        free = tile([P, 3, T], F32, "wide1")
+        got[1] = [free[:, 2, :]]
         fetch(1, 0, 0, T)
+        expert(2, 0)
+        quantize_w(4)
+        expert(2, 1)
+        expert(2, 2)
+        quantize_w(5, 0, 4)
+        quantize_w(5, 4, 6)
+        for e in range(3, E):
+            expert(2, e)
+        held = tile([P, 4, T], F32, "narrow")
+        got[0].extend([held[:, 3, :], held[:, 2, :]])
+        got[1].extend([held[:, 0, :], held[:, 1, :], free[:, 0, :], free[:, 1, :]])
+        add_two(nc.gpsimd, 0)
+        add_third(nc.gpsimd, 0, 0, T)
         fetch(1, 1, 0, T)
         add_two(nc.gpsimd, 1)
         fetch(1, 2, 0, T)
         add_third(nc.gpsimd, 1, 0, T)
         cut = 320
-        room(2, "x0_2", "x0_3")
+        last = tile([P, 4, T], F32, "gate_b")
+        got[2] = [last[:, r, :] for r in range(4)] + [last[:, 0, :]]
         fetch(2, 0, 0, T)
         fetch(2, 1, 0, T)
-        add_two(nc.gpsimd, 2)
+        add_two(nc.gpsimd, 2, 0, cut)
+        add_two(nc.gpsimd, 2, cut, T)
         fetch(2, 2, 0, cut)
         fetch(2, 2, cut, T)
         add_third(nc.vector, 2, 0, cut)

@@ -41,7 +41,7 @@ def tile_moe_pre_lin_bias_kernel(tc, xT, w, b, gate, offs, pos1, pos2, pos3, out
         gate_b = tile([P, 2 * PAIR], F32, "gate_b")
         bias_sb = tile([P, NT, 8], F32, "bias")
         planes = [[tile([P, 2 * PAIR + PAD], F32, "x%d_%d" % (g, t)) for t in range(PACK)] for g in range(PASSES)]
-        SPLIT = 0
+        SPLIT = 1
         w_ab = [tile([P, PACK, N if i < SPLIT else 2 * P], F32, "w%d" % i) for i in range(PASSES * E)]
         w_c = {i: tile([P, PACK, P], F32, "wc%d" % i) for i in range(SPLIT, PASSES * E)}
         x_codes = tile([P, PASSES, S], U32, "x_codes")
@@ -180,10 +180,8 @@ def tile_moe_pre_lin_bias_kernel(tc, xT, w, b, gate, offs, pos1, pos2, pos3, out
         load_plane(0, 0)
         load_gate(0, PAIR)
         load_plane(0, 1)
-        load_w(0, 0 * P, 1 * P)
         load_plane(0, 2)
-        load_w(0, 1 * P, 2 * P)
-        load_w(0, 2 * P, 3 * P)
+        load_w(0, 0, N)
         load_plane(0, 3)
         load_gate(PAIR, S)
         load_w(1, 0, 2 * P)

from contextlib import ExitStack

import concourse.mybir as mybir

K, T, E, C, N = 1024, 512, 6, 256, 384
S = E * C
P = 128
PACK = 4
PASSES = K // (P * PACK)
NT = N // P
PAD = 16
PAIR = 2 * C

F32 = mybir.dt.float32
BF16 = mybir.dt.bfloat16
U32 = mybir.dt.uint32
U16 = mybir.dt.uint16
U8 = mybir.dt.uint8
FP8X4 = mybir.dt.float8_e4m3fn_x4
MULT = mybir.AluOpType.mult
ADD = mybir.AluOpType.add
IDENT = mybir.ActivationFunctionType.Identity

FLOPS = 2 * S * K * N
BYTES = 4 * (K * T + E * K * N + N * E + S + N * T) + 2 * P * (S + 3 * T) // 16


def tile_moe_pre_lin_bias_kernel(tc, xT, w, b, gate, offs, pos1, pos2, pos3, out):
    nc = tc.nc
    with ExitStack() as ctx:
        lists = ctx.enter_context(tc.tile_pool(name="lists", bufs=1))
        keep = ctx.enter_context(tc.tile_pool(name="keep", bufs=1))
        psum = ctx.enter_context(tc.psum_pool(name="psum", bufs=8))

        def tile(shape, dtype, tag):
            return keep.tile(shape, dtype, name=tag, tag=tag, align_bytes=64)

        offs_sb = lists.tile([P, S // 16], U16, name="offs_sb")
        pos_sb = [lists.tile([P, T // 16], U16, name="pos%d_sb" % r) for r in range(3)]
        gate_a = tile([P, PAIR], F32, "gate_a")
        gate_b = tile([P, 2 * PAIR], F32, "gate_b")
        bias_sb = tile([P, NT, 8], F32, "bias")
        planes = [[tile([P, 2 * PAIR + PAD], F32, "x%d_%d" % (g, t)) for t in range(PACK)] for g in range(PASSES)]
        SPLIT = 1
        w_ab = [tile([P, PACK, N if i < SPLIT else 2 * P], F32, "w%d" % i) for i in range(PASSES * E)]
        w_c = {i: tile([P, PACK, P], F32, "wc%d" % i) for i in range(SPLIT, PASSES * E)}
        x_codes = tile([P, PASSES, S], U32, "x_codes")
        x_scales = tile([P, PASSES, S], U8, "x_scales")
        y = [tile([P, S], F32, "y%d" % nt) for nt in range(NT)]
        narrow = {0: tile([P, PACK, PAIR], F32, "narrow")}
        wide = [tile([P, PACK, 2 * PAIR], F32, "wide%d" % g) for g in range(PASSES)]
        x_bf, w_bf, w_codes, w_scales, got = {}, {}, {}, {}, {}

        x_rows = xT.rearrange("(g p t) c -> g t p c", p=P, t=PACK)
        w_rows = w.rearrange("e (g p j) n -> g e p j n", p=P, j=PACK)

        def load_plane(g, t):
            nc.sync.dma_start(out=planes[g][t][:, :T], in_=x_rows[g, t])

        def gate_of(lo, hi):
            return gate_a[:, lo:hi] if lo < PAIR else gate_b[:, lo - PAIR : hi - PAIR]

        def load_gate(lo, hi):
            nc.sync.dma_start(out=gate_of(lo, hi), in_=gate[:P, lo:hi])

        def raw(i, lo, hi):
            return w_c[i][:, :, lo - 2 * P : hi - 2 * P] if i >= SPLIT and lo >= 2 * P else w_ab[i][:, :, lo:hi]

        def load_w(i, lo, hi):
            nc.sync.dma_start(out=raw(i, lo, hi), in_=w_rows[i // E, i % E][:, :, lo:hi])

        def prod(g, lo, hi):
            if lo >= PAIR:
                return wide[g][:, :, lo - PAIR : hi - PAIR]
            if g not in narrow:
                narrow[g] = tile([P, PACK, PAIR], F32, "gate_b")
            return narrow[g][:, :, lo:hi]

        def gather(g, t, lo, hi):
            nc.vector.tensor_tensor(
                prod(g, lo, hi)[:, t, :],
                planes[g][t][:].indirect(offs_sb[:, lo // 16 : hi // 16]),
                gate_of(lo, hi),
                MULT,
            )

        def gather_x(g, lo, hi):
            for t in range(PACK):
                gather(g, t, lo, hi)

        x_tag = {(0, False): "xbf", (0, True): "w6", (1, True): "narrow", (1, False): "xbf"}

        def rounded(g, lo, hi):
            key = (g, lo >= PAIR)
            if key not in x_bf:
                x_bf[key] = tile([P, 2 * PAIR if key[1] else PAIR, PACK], BF16, x_tag[key])
            base = PAIR if key[1] else 0
            return x_bf[key][:, lo - base : hi - base, :]

        def round_x(g, lo, hi):
            nc.scalar.copy(
                out=rounded(g, lo, hi).rearrange("p (c i) t -> p c t i", i=4),
                in_=prod(g, lo, hi).rearrange("p t (c i) -> p c t i", i=4),
            )

        def q_x(g, lo, hi):
            nc.vector.quantize_mx(
                out=x_codes[:, g, lo:hi].bitcast(FP8X4),
                scales=x_scales[:, g, lo:hi],
                in_=rounded(g, lo, hi).rearrange("p c t -> p (c t)"),
            )

        batches = [
            ([(0, i) for i in range(8)], "b0", "x1_0"),
            ([(1, i) for i in range(8)], "b1", "xbf"),
            ([(nt, i) for nt in (0, 1) for i in range(8, 12)], "wide0", "x1_1"),
            ([(2, i) for i in (0, 6)], "b3", "b1"),
            ([(2, i) for i in (1, 7, 2, 8)], "b3", "x1_2"),
            ([(2, i) for i in (3, 9, 4, 10, 5, 11)], "narrow", "x1_3"),
        ]
        place = {block: (n, at * P) for n, batch in enumerate(batches) for at, block in enumerate(batch[0])}

        def w_target(nt, i):
            n, at = place[(nt, i)]
            if n not in w_bf:
                w_bf[n] = tile([P, len(batches[n][0]) * P, PACK], BF16, batches[n][1])
            return w_bf[n][:, at : at + P, :]

        def cast_w(i, tiles, copy=nc.scalar.copy):
            for nt in tiles:
                copy(
                    out=w_target(nt, i).rearrange("p (c i) j -> p c j i", i=4),
                    in_=raw(i, nt * P, (nt + 1) * P).rearrange("p j (c i) -> p c j i", i=4),
                )

        def cast_w_gpsimd(i, nt):
            nc.gpsimd.tensor_scalar(
                w_target(nt, i), raw(i, nt * P, (nt + 1) * P).rearrange("p j c -> p c j"), 1.0, 0.0, MULT, ADD
            )

        def quantize_w(n, lo=0, hi=None):
            width = len(batches[n][0]) * P
            if n not in w_codes:
                w_codes[n] = tile([P, width], U32, batches[n][2])
                w_scales[n] = tile([P, width], U8, "ws%d" % n)
            cols = slice(lo * P, hi * P if hi else width)
            nc.vector.quantize_mx(
                out=w_codes[n][:, cols].bitcast(FP8X4),
                scales=w_scales[n][:, cols],
                in_=w_bf[n][:, cols, :].rearrange("p c j -> p (c j)"),
            )

        def expert(nt, e):
            acc = psum.tile([P, C], F32, name="acc")
            slots = slice(e * C, (e + 1) * C)
            for g in range(PASSES):
                n, at = place[(nt, g * E + e)]
                nc.tensor.matmul_mx(
                    out=acc[:],
                    lhsT=w_codes[n][:, at : at + P].bitcast(FP8X4),
                    lhsT_scale=w_scales[n][:, at : at + P],
                    rhs=x_codes[:, g, slots].bitcast(FP8X4),
                    rhs_scale=x_scales[:, g, slots],
                    start=(g == 0),
                    stop=(g == PASSES - 1),
                )
            nc.scalar.activation(out=y[nt][:, slots], in_=acc[:], func=IDENT, bias=bias_sb[:, nt, e : e + 1])

        def fetch(nt, r, a, z):
            nc.vector.tensor_copy(got[nt][r][:, a:z], y[nt][:].indirect(pos_sb[r][:, a // 16 : z // 16]))

        def add_two(adder, nt, a=0, z=T):
            adder.tensor_tensor(got[nt][3][:, a:z], got[nt][0][:, a:z], got[nt][1][:, a:z], ADD)

        def add_third(adder, nt, a, z):
            adder.tensor_tensor(got[nt][4][:, a:z], got[nt][3][:, a:z], got[nt][2][:, a:z], ADD)
            nc.sync.dma_start(out=out[nt * P : (nt + 1) * P, a:z], in_=got[nt][4][:, a:z])

        nc.sync.dma_start(offs_sb[:], offs)
        load_plane(0, 0)
        load_gate(0, PAIR)
        load_plane(0, 1)
        load_plane(0, 2)
        load_w(0, 0, N)
        load_plane(0, 3)
        load_gate(PAIR, S)
        load_w(1, 0, 2 * P)
        load_w(2, 0, 2 * P)
        load_w(3, 0, 2 * P)
        load_w(4, 0, 2 * P)
        load_plane(1, 0)
        load_w(5, 0, 2 * P)
        load_w(6, 0, 2 * P)
        load_plane(1, 1)
        load_w(6, 2 * P, 3 * P)
        load_w(7, 0, 2 * P)
        load_plane(1, 2)
        load_w(8, 0, 2 * P)
        load_w(9, 0, 2 * P)
        load_plane(1, 3)
        load_w(10, 0, 2 * P)
        load_w(11, 0, 2 * P)
        nc.sync.dma_start(out=bias_sb[:, :, :E], in_=b.rearrange("(c p) e -> p c e", p=P))
        nc.sync.dma_start(pos_sb[0][:], pos1)
        nc.sync.dma_start(pos_sb[1][:], pos2)
        nc.sync.dma_start(pos_sb[2][:], pos3)
        load_w(1, 2 * P, 3 * P)
        load_w(7, 2 * P, 3 * P)
        load_w(2, 2 * P, 3 * P)
        load_w(8, 2 * P, 3 * P)
        load_w(3, 2 * P, 3 * P)
        load_w(9, 2 * P, 3 * P)
        load_w(4, 2 * P, 3 * P)
        load_w(10, 2 * P, 3 * P)
        load_w(5, 2 * P, 3 * P)
        load_w(11, 2 * P, 3 * P)

        gather_x(0, 0, PAIR)
        cast_w(0, [0, 1, 2])
        round_x(0, 0, PAIR)
        gather_x(0, PAIR, S)
        q_x(0, 0, PAIR)
        for i in range(1, 7):
            cast_w(i, [0, 1])
        round_x(0, PAIR, 2 * PAIR)
        round_x(0, 2 * PAIR, S)
        cast_w(6, [2])
        gather(1, 0, PAIR, S)
        gather(1, 1, PAIR, S)
        q_x(0, PAIR, 2 * PAIR)
        gather(1, 2, PAIR, S)
        q_x(0, 2 * PAIR, S)
        gather(1, 3, PAIR, S)
        for i in range(7, 12):
            cast_w(i, [0, 1, 2] if i == 6 else [0, 1])
        round_x(1, PAIR, 2 * PAIR)
        round_x(1, 2 * PAIR, S)
        gather_x(1, 0, PAIR)
        quantize_w(0)
        quantize_w(2)
        q_x(1, PAIR, 2 * PAIR)
        q_x(1, 2 * PAIR, S)
        round_x(1, 0, C)
        round_x(1, C, PAIR)
        for e in range(2, E):
            expert(0, e)
        q_x(1, 0, C)
        expert(0, 0)
        q_x(1, C, PAIR)
        expert(0, 1)
        quantize_w(1)
        quantize_w(3)
        for e in range(E):
            expert(1, e)
        for i in (1, 7, 2, 8):
            cast_w_gpsimd(i, 2)
        for i in (3, 9, 4, 10, 5, 11):
            cast_w(i, [2])
        first = tile([P, 3, T], F32, "wide0")
        got[0] = [first[:, r, :] for r in range(3)]
        for r in range(3):
            fetch(0, r, 0, T)
        free = tile([P, 3, T], F32, "wide1")
        got[1] = [free[:, 2, :]]
        fetch(1, 0, 0, T)
        expert(2, 0)
        quantize_w(4)
        expert(2, 1)
        expert(2, 2)
        quantize_w(5, 0, 4)
        quantize_w(5, 4, 6)
        for e in range(3, E):
            expert(2, e)
        held = tile([P, 4, T], F32, "narrow")
        got[0].extend([held[:, 3, :], held[:, 2, :]])
        got[1].extend([held[:, 0, :], held[:, 1, :], free[:, 0, :], free[:, 1, :]])
        add_two(nc.gpsimd, 0)
        add_third(nc.gpsimd, 0, 0, T)
        fetch(1, 1, 0, T)
        add_two(nc.gpsimd, 1)
        fetch(1, 2, 0, T)
        add_third(nc.gpsimd, 1, 0, T)
        cut = 320
        last = tile([P, 4, T], F32, "gate_b")
        got[2] = [last[:, r, :] for r in range(4)] + [last[:, 0, :]]
        fetch(2, 0, 0, T)
        fetch(2, 1, 0, T)
        add_two(nc.gpsimd, 2, 0, cut)
        add_two(nc.gpsimd, 2, cut, T)
        fetch(2, 2, 0, cut)
        fetch(2, 2, cut, T)
        add_third(nc.vector, 2, 0, cut)
        add_third(nc.vector, 2, cut, T)
